import numpy as np
import ml_dtypes


def mxq(x, axis, fmt="e4m3"):
    dtype, down = {"e4m3": (ml_dtypes.float8_e4m3fn, 7), "e5m2": (ml_dtypes.float8_e5m2, 14)}[fmt]
    v = np.moveaxis(np.asarray(x, np.float32).astype(ml_dtypes.bfloat16).astype(np.float64), axis, -1)
    blocks = v.reshape(v.shape[:-1] + (-1, 32))
    amax = np.abs(blocks).max(-1, keepdims=True)
    byte = np.maximum(np.where(amax > 0, np.frexp(amax)[1] - 1 + 127, 0) - down, 1)
    scale = np.exp2(byte - 127.0)
    codes = (blocks / scale).astype(np.float32).astype(dtype).astype(np.float64)
    return np.moveaxis((codes * scale).reshape(v.shape), -1, axis)


WIDE = False


def mx_kscale(k):
    if not WIDE:
        return np.ones(k)
    levels = np.array([10, -10, 5, -5, 0])
    if k % 512:
        return np.exp2(np.random.permutation(np.resize(levels, k // 32))).repeat(32)
    a = np.empty((k // 512, 16))
    for p in range(k // 512):
        a[p, :8] = np.random.permutation(np.resize(levels, 8))
        for g in range(8):
            far = levels[np.abs(levels - a[p, g]) >= 10]
            a[p, g + 8] = far[np.random.randint(len(far))]
    return np.exp2(a.ravel()).repeat(32)


def f64(x):
    return np.asarray(x).astype(np.float64)


def striped(idx):
    return np.tile(idx.reshape(-1, 16).T, (8, 1)).astype(np.uint16)


def unstriped(offs):
    return offs[:16].T.reshape(-1).astype(np.int64)


E2M1 = np.array([0.0, 0.5, 1.0, 1.5, 2.0, 3.0, 4.0, 6.0, -0.0, -0.5, -1.0, -1.5, -2.0, -3.0, -4.0, -6.0])


def pack_weight(w, fmt):
    k, n = w.shape
    w = f64(np.asarray(w, np.float32).astype(ml_dtypes.bfloat16)).reshape(k // 32, 32, n)
    amax = np.abs(w).max(1)
    if fmt == "e4m3":
        byte = np.frexp(amax)[1] - 1 + 127 - 7
    else:
        mant, ex = np.frexp(amax / 6.0)
        byte = np.where(mant > 0.5, ex, ex - 1) + 127
    byte = np.clip(np.where(amax > 0, byte, 1), 1, 254)
    scaled = (w * np.exp2(127.0 - byte)[:, None, :]).reshape(k, n).astype(np.float32)
    by_word = np.ascontiguousarray(scaled.reshape(k // 512, 128, 4, n).transpose(0, 1, 3, 2))
    if fmt == "e4m3":
        words = by_word.astype(ml_dtypes.float8_e4m3fn).view(np.uint8)
    else:
        c = by_word.astype(ml_dtypes.float4_e2m1fn).view(np.uint8) & 0xF
        words = (c[..., 0::2] | (c[..., 1::2] << 4)).reshape(k // 512, 128, 2 * n)
    return np.ascontiguousarray(words), np.ascontiguousarray(byte.astype(np.uint8).reshape(k // 512, 16, n))


def unpack_weight(words, scales, fmt):
    g, _, n = scales.shape
    words = np.ascontiguousarray(words).reshape(g, 128, n, -1)
    if fmt == "e4m3":
        vals = words.view(ml_dtypes.float8_e4m3fn).astype(np.float64)
    else:
        nib = np.empty((g, 128, n, 4), np.uint8)
        nib[..., 0::2] = words & 0xF
        nib[..., 1::2] = words >> 4
        vals = E2M1[nib]
    vals = vals * np.repeat(np.exp2(scales.astype(np.float64) - 127.0), 8, axis=1)[..., None]
    return vals.transpose(0, 1, 3, 2).reshape(g * 512, n)


def gelu(v):
    return 0.5 * v * (1.0 + np.tanh(np.sqrt(2.0 / np.pi) * (v + 0.044715 * v**3)))


K, K2, M, T, TC, S, H, T2, P, N = 1024, 512, 512, 2048, 1024, 512, 1024, 2048, 1024, 512

def setup_inputs():
    n = np.random.standard_normal
    s, s2, s3, u = mx_kscale(K)[:, None], mx_kscale(K2)[:, None], mx_kscale(M)[:, None], mx_kscale(H)[:, None]
    d = {}
    d["tab_words"], d["tab_scales"] = pack_weight(n((K, T)) * s, "e4m3")
    d["tab2_words"], d["tab2_scales"] = pack_weight(n((K2, TC)) * s2, "e4m3")
    d["offs"] = striped(np.random.permutation(T)[:S])
    d["offs2"] = striped(np.random.permutation(TC)[:S])
    perm = np.random.permutation(T2)
    d["offs3"] = striped(perm[:S])
    d["offs4"] = striped(perm[S:2 * S])
    d["offs5"] = striped(np.random.permutation(T2)[:P])
    d["w1"] = (1.6 * n((K, H)) / K**0.5 / s).astype(np.float32)
    d["b1"] = (0.8 * n(H)).astype(np.float32)
    d["w2_words"], d["w2_scales"] = pack_weight(2.0 * n((K2, H)) / K2**0.5 / s2, "e4m3")
    d["wg1"] = np.exp(0.3 * n((128, S))).astype(np.float32)
    d["wg2"] = np.exp(0.3 * n((128, S))).astype(np.float32)
    d["page0"] = (0.8 * n((H, T2))).astype(np.float32)
    d["gain"] = (np.exp(0.4 * n(H)) * u[:, 0]).astype(np.float32)
    d["w3_words"], d["w3_scales"] = pack_weight(n((H, N)) / H**0.5 / u, "e2m1")
    d["safe"] = (n((M, P)) * s3).astype(np.float32)
    d["w4"] = (n((M, N)) / M**0.5 / s3).astype(np.float32)
    return d

def reference(tab_words, tab_scales, tab2_words, tab2_scales, offs, offs2, offs3, offs4, offs5, w1, b1, w2_words, w2_scales, wg1, wg2, page0, gain, w3_words, w3_scales, safe, w4):
    v = unpack_weight(tab_words, tab_scales, "e4m3")[:, unstriped(offs)]
    v2 = unpack_weight(tab2_words, tab2_scales, "e4m3")[:, unstriped(offs2)]
    h1 = np.tanh((mxq(f64(w1), 0, "e4m3").T @ v) + f64(b1)[:, None])
    cue = unpack_weight(w2_words, w2_scales, "e4m3").T @ v2
    h2 = cue / (1.0 + np.exp(-cue))
    page = f64(page0).copy()
    page[:, unstriped(offs3)] = np.tile(f64(wg1), (H // 128, 1)) * h1
    page[:, unstriped(offs4)] = np.tile(f64(wg2), (H // 128, 1)) * h2
    x = page[:, unstriped(offs5)] * f64(gain)[:, None]
    y = unpack_weight(w3_words, w3_scales, "e2m1").T @ mxq(x, 0, "e4m3")
    shot = mxq(f64(w4), 0, "e4m3").T @ mxq(f64(safe), 0, "e4m3")
    return np.minimum(y, shot)

@@ -1,0 +1,310 @@
+from contextlib import ExitStack
+
+import concourse.mybir as mybir
+
+F32 = mybir.dt.float32
+BF16 = mybir.dt.bfloat16
+I32 = mybir.dt.int32
+U32 = mybir.dt.uint32
+U16 = mybir.dt.uint16
+U8 = mybir.dt.uint8
+FP8X4 = mybir.dt.float8_e4m3fn_x4
+FP4X4 = mybir.dt.float4_e2m1fn_x4
+ACT = mybir.ActivationFunctionType
+ALU = mybir.AluOpType
+
+FLOPS = 3221225472
+
+P = 128
+PACK = 4
+KP = 512
+T, TC, S, T2, PJ = 2048, 1024, 512, 2048, 1024
+
+
+def tile_list_snooker_visit_board_kernel(
+    tc, tab_words, tab_scales, tab2_words, tab2_scales, offs, offs2, offs3, offs4, offs5,
+    w1, b1, w2_words, w2_scales, wg1, wg2, page0, gain, w3_words, w3_scales, safe, w4, out,
+):
+    nc = tc.nc
+    with ExitStack() as ctx:
+        lists = ctx.enter_context(tc.tile_pool(name="lists", bufs=1))
+        keep = ctx.enter_context(tc.tile_pool(name="keep", bufs=1))
+        psum = ctx.enter_context(tc.psum_pool(name="psum", bufs=8))
+
+        def load_list(src, name):
+            tile = lists.tile([P, src.shape[1]], U16, name=name)
+            nc.sync.dma_start(tile[:], src)
+            return tile
+
+        def held(shape, dtype, name, tag=None):
+            return keep.tile(shape, dtype, name=name, tag=tag or name, bufs=1, align_bytes=64)
+
+        def ring(shape, dtype, tag, bufs):
+            return keep.tile(shape, dtype, name=tag, tag=tag, bufs=bufs, align_bytes=64)
+
+        def raw_tile(shape, dtype):
+            return ring(shape, dtype, "raw", 4)
+
+        def grouped_tile(shape):
+            return ring(shape, BF16, "grouped", 4)
+
+        def bank():
+            return psum.tile([P, KP], F32, name="bank", tag="bank")
+
+        def zeroed_plane(engine, width, name):
+            tile = held([P, width], U8, name)
+            engine.memset(tile[:].bitcast(I32), 0)
+            return tile
+
+        def load_words(src, name):
+            tile = held([P, src.shape[1]], I32, name)
+            nc.sync.dma_start(tile[:], src.rearrange("p t i -> p (t i)").bitcast(I32))
+            return tile
+
+        def gather(window, offsets, dtype, name):
+            tile = held([P, S], dtype, name)
+            nc.vector.tensor_copy(tile[:], window.indirect(offsets[:]))
+            return tile
+
+        def quantize(grouped, width):
+            codes = ring([P, width], U32, "codes", 5)
+            scales = ring([P, width], U8, "scales", 5)
+            nc.vector.quantize_mx(out=codes[:].bitcast(FP8X4), scales=scales[:], in_=grouped)
+            return codes, scales
+
+        def load_raw(src):
+            raw = raw_tile([P, PACK, KP], F32)
+            nc.sync.dma_start(raw[:], src.rearrange("(p j) c -> p j c", j=PACK))
+            return raw
+
+        def interleave(copy, grouped, planes):
+            copy(
+                grouped.rearrange("p (c i t) -> p c t i", i=4, t=PACK),
+                planes.rearrange("p t (c i) -> p c t i", i=4),
+            )
+
+        def interleave_dealt(grouped, raw):
+            nc.scalar.copy(
+                grouped.rearrange("p (t m j) -> p m j t", t=PACK, j=PACK),
+                raw.rearrange("p j (m t) -> p m j t", t=PACK),
+            )
+
+        def load_wg(wg, slots, name, tag=None):
+            tile = held([P, slots.stop - slots.start, S], F32, name, tag)
+            rows = wg.rearrange("(q t) s -> q t s", t=PACK)
+            for quad in range(4):
+                nc.sync.dma_start(tile[32 * quad : 32 * quad + 32], rows[:, slots, :])
+            return tile
+
+        page_rows = page0.rearrange("(a p t) c -> a t p c", a=2, t=PACK)
+        pages = {}
+
+        def load_page(u):
+            pages[u] = held([P, T2], F32, "page%d" % u)
+            nc.sync.dma_start(pages[u][:], page_rows[u // PACK, u % PACK])
+
+        def scatter(u, offsets, h, wg_row):
+            nc.vector.tensor_tensor(pages[u][:].indirect(offsets[:]), h[:], wg_row, ALU.mult)
+
+        t2_plane = zeroed_plane(nc.vector, TC, "t2_plane")
+        w2_plane_raw = zeroed_plane(nc.vector, KP, "w2_plane_raw")
+        tab_plane = zeroed_plane(nc.gpsimd, T, "tab_plane")
+        w3_plane = zeroed_plane(nc.gpsimd, 2 * KP, "w3_plane")
+
+        list2 = load_list(offs2, "list2")
+        t2_words = load_words(tab2_words[0], "t2_words")
+        for quad in range(4):
+            nc.sync.dma_start(
+                t2_plane[32 * quad : 32 * quad + 4, :].bitcast(I32),
+                tab2_scales[0, 4 * quad : 4 * quad + 4, :].bitcast(I32),
+            )
+        w2_raw = [load_words(w2_words[0, :, 0:KP, :], "w2_raw0")]
+        for quad in range(4):
+            nc.sync.dma_start(
+                w2_plane_raw[32 * quad : 32 * quad + 8, :].bitcast(I32),
+                w2_scales[0, 4 * quad : 4 * quad + 4, :].rearrange("r (b c) -> b r c", b=2).bitcast(I32),
+            )
+        list4 = load_list(offs4, "list4")
+        wg2_first = load_wg(wg2, slice(0, 1), "wg2_first")
+        load_page(0)
+        w2_raw.append(load_words(w2_words[0, :, KP : 2 * KP, :], "w2_raw1"))
+        wg2_rest = load_wg(wg2, slice(1, 4), "wg2_rest", "wg2_then_shot")
+
+        v2_words = gather(t2_words[:].bitcast(U32), list2, U32, "v2_words")
+        v2_plane = gather(t2_plane[:], list2, U8, "v2_plane")
+        w2_plane = held([P, KP], U8, "w2_plane")
+        nc.vector.tensor_copy(w2_plane[:].rearrange("p (t m) -> p m t", t=PACK), w2_plane_raw[:].rearrange("p (m t) -> p m t", t=PACK))
+
+        def cue_features(b):
+            dealt = held([P, KP], I32, "w2_dealt%d" % b)
+            nc.vector.tensor_copy(dealt[:].rearrange("p (t m) -> p m t", t=PACK), w2_raw[b][:].rearrange("p (m t) -> p m t", t=PACK))
+            tiles = []
+            for t in range(PACK):
+                cols = slice(P * t, P * (t + 1))
+                acc = bank()
+                nc.tensor.matmul_mx(
+                    out=acc[:], lhsT=dealt[:, cols].bitcast(FP8X4), lhsT_scale=w2_plane[4 * b :, cols],
+                    rhs=v2_words[:].bitcast(FP8X4), rhs_scale=v2_plane[:], start=True, stop=True,
+                )
+                h = ring([P, S], F32, "h", 6)
+                nc.scalar.activation(h[:], acc[:], ACT.Silu)
+                tiles.append(h)
+            return tiles
+
+        def wg2_row(t):
+            return wg2_first[:, 0, :] if t == 0 else wg2_rest[:, t - 1, :]
+
+        h2 = cue_features(0)
+        scatter(0, list4, h2[0], wg2_row(0))
+        h2 = h2 + cue_features(1)
+        for u in range(1, 4):
+            load_page(u)
+            scatter(u, list4, h2[u], wg2_row(u))
+
+        list1 = load_list(offs, "list1")
+        for quad in range(4):
+            nc.sync.dma_start(
+                tab_plane[32 * quad : 32 * quad + 8, :].bitcast(I32),
+                tab_scales[:, 4 * quad : 4 * quad + 4, :].bitcast(I32),
+            )
+        v_plane = gather(tab_plane[:], list1, U8, "v_plane")
+        v_words = []
+        for a in range(2):
+            words = load_words(tab_words[a], "tab_words%d" % a)
+            v_words.append(gather(words[:].bitcast(U32), list1, U32, "v_words%d" % a))
+            load_page(4 + a)
+            scatter(4 + a, list4, h2[4 + a], wg2_row(a))
+
+        bias = held([P, 2, PACK], F32, "bias")
+        nc.sync.dma_start(bias[:], b1.rearrange("(a p t) -> p a t", a=2, t=PACK))
+
+        def w1_piece(a, b, grouped):
+            raw = load_raw(w1[KP * a : KP * (a + 1), KP * b : KP * (b + 1)])
+            interleave_dealt(grouped, raw[:])
+            return quantize(grouped, KP)
+
+        def layout_features(b, w1q):
+            tiles = []
+            for t in range(PACK):
+                cols = slice(P * t, P * (t + 1))
+                acc = bank()
+                for a in range(2):
+                    codes, scales = w1q[a]
+                    nc.tensor.matmul_mx(
+                        out=acc[:], lhsT=codes[:, cols].bitcast(FP8X4), lhsT_scale=scales[:, cols],
+                        rhs=v_words[a][:].bitcast(FP8X4), rhs_scale=v_plane[4 * a :, :],
+                        start=(a == 0), stop=(a == 1),
+                    )
+                h = ring([P, S], F32, "h", 6)
+                nc.scalar.activation(h[:], acc[:], ACT.Tanh, bias=bias[:, b, t : t + 1])
+                tiles.append(h)
+            return tiles
+
+        w1q = [w1_piece(a, 0, grouped_tile([P, PACK * KP])[:]) for a in range(2)]
+        h1 = layout_features(0, w1q)
+        for u in range(6, 8):
+            load_page(u)
+            scatter(u, list4, h2[u], wg2_row(u - 4))
+        list3 = load_list(offs3, "list3")
+        wg1_rows = load_wg(wg1, slice(0, 4), "wg1_rows")
+        for u in range(4):
+            scatter(u, list3, h1[u], wg1_rows[:, u, :])
+
+        def plain_piece(src):
+            raw = load_raw(src)
+            grouped = grouped_tile([P, PACK * KP])
+            interleave(nc.scalar.copy, grouped[:], raw[:])
+            return quantize(grouped[:], KP)
+
+        w4q = plain_piece(w4)
+        safeq = [plain_piece(safe[:, KP * half : KP * (half + 1)]) for half in range(2)]
+        last_grouped = held([P, PACK * KP], BF16, "last_grouped", "w1_then_picks")
+        w1q = [w1_piece(0, 1, grouped_tile([P, PACK * KP])[:]), w1_piece(1, 1, last_grouped[:])]
+
+        w3_codes = held([P, 2, 2 * KP], U8, "w3_codes")
+        nc.sync.dma_start(w3_codes[:].bitcast(I32), w3_words.rearrange("a p c -> p a c").bitcast(I32))
+        w3_view = w3_plane[:].rearrange("p (a c) -> p a c", a=2)
+        for quad in range(4):
+            nc.sync.dma_start(
+                w3_view[32 * quad : 32 * quad + 4].bitcast(I32),
+                w3_scales[:, 4 * quad : 4 * quad + 4, :].rearrange("a r c -> r a c").bitcast(I32),
+            )
+        gains = held([P, 2, PACK], F32, "gains")
+        nc.sync.dma_start(gains[:], gain.rearrange("(a p t) -> p a t", a=2, t=PACK))
+        list5 = load_list(offs5, "list5")
+
+        h1 = h1 + layout_features(1, w1q)
+
+        shots = [held([P, 4, KP], F32, "shot0"), held([P, 4, KP], F32, "shot1", "wg2_then_shot")]
+        for half in range(2):
+            for c in range(4):
+                cols = slice(P * c, P * (c + 1))
+                acc = bank()
+                nc.tensor.matmul_mx(
+                    out=acc[:], lhsT=w4q[0][:, cols].bitcast(FP8X4), lhsT_scale=w4q[1][:, cols],
+                    rhs=safeq[half][0][:].bitcast(FP8X4), rhs_scale=safeq[half][1][:], start=True, stop=True,
+                )
+                nc.scalar.copy(shots[half][:, c, :], acc[:])
+
+        def pick(u, picks, scaled, j0, width):
+            a, t = divmod(u, PACK)
+            nc.vector.tensor_copy(picks[:, t, :], pages[u][:].indirect(list5[:, j0 // 16 : (j0 + width) // 16]))
+            nc.scalar.activation(scaled[:, t, :], picks[:, t, :], ACT.Copy, scale=gains[:, a, t : t + 1])
+
+        picks0 = held([P, PACK, PJ], F32, "picks0", "w1_then_picks")
+        scaled0 = raw_tile([P, PACK, PJ], BF16)
+        for u in range(4):
+            pick(u, picks0, scaled0, 0, PJ)
+        grouped0 = raw_tile([P, 2, PACK * KP], BF16)
+        for half in range(2):
+            interleave(nc.scalar.copy, grouped0[:, half, :], scaled0[:, :, KP * half : KP * (half + 1)])
+
+        picks_a = raw_tile([P, PACK, KP], F32)
+        scaled_a = grouped_tile([P, PACK, KP])
+        for u in range(4, 8):
+            scatter(u, list3, h1[u], wg1_rows[:, u - 4, :])
+            pick(u, picks_a, scaled_a, 0, KP)
+        grouped_a = held([P, PACK * KP], BF16, "grouped_a", "a_then_picks")
+        interleave(nc.scalar.copy, grouped_a[:], scaled_a[:])
+
+        def scores(x0, x0_col, x1, j0, width, n_cols):
+            half, col = divmod(j0, KP)
+            for c in range(4):
+                acc = bank()
+                for n0 in range(0, width, n_cols):
+                    for a, (xq, base) in enumerate(((x0, x0_col), (x1, 0))):
+                        cols = slice(base + n0, base + n0 + n_cols)
+                        nc.tensor.matmul_mx(
+                            out=acc[:, n0 : n0 + n_cols],
+                            lhsT=w3_codes[:, a, 2 * P * c : 2 * P * (c + 1)].bitcast(FP4X4),
+                            lhsT_scale=w3_view[:, a, P * c : P * (c + 1)],
+                            rhs=xq[0][:, cols].bitcast(FP8X4), rhs_scale=xq[1][:, cols],
+                            start=(a == 0), stop=(a == 1),
+                        )
+                shot = shots[half][:, c, col : col + width]
+                nc.vector.tensor_tensor(shot, acc[:, 0:width], shot, ALU.min)
+                nc.sync.dma_start(out[P * c : P * (c + 1), j0 : j0 + width], shot)
+
+        Q = KP // 2
+        picks_b = raw_tile([P, PACK, Q], F32)
+        scaled_b = grouped_tile([P, PACK, Q])
+        for u in range(4, 8):
+            pick(u, picks_b, scaled_b, KP, Q)
+        grouped_b = grouped_tile([P, PACK * Q])
+        interleave(nc.scalar.copy, grouped_b[:], scaled_b[:])
+
+        x0 = [quantize(grouped0[:, half, :], KP) for half in range(2)]
+        xa = quantize(grouped_a[:], KP)
+
+        picks_c = held([P, PACK, Q], F32, "picks_c", "a_then_picks")
+        scaled_c = grouped_tile([P, PACK, Q])
+        for u in range(4, 8):
+            pick(u, picks_c, scaled_c, KP + Q, Q)
+
+        scores(x0[0], 0, xa, 0, KP, KP)
+        xb = quantize(grouped_b[:], Q)
+        grouped_c = grouped_tile([P, PACK * Q])
+        interleave(nc.vector.tensor_copy, grouped_c[:], scaled_c[:])
+        xc = quantize(grouped_c[:], Q)
+        scores(x0[1], 0, xb, KP, Q, P)
+        scores(x0[1], Q, xc, KP + Q, Q, P)

@@ -1,6 +1,7 @@
 from contextlib import ExitStack
 
 import concourse.mybir as mybir
+from concourse.masks import make_identity
 
 F32 = mybir.dt.float32
 BF16 = mybir.dt.bfloat16
@@ -89,12 +90,25 @@ def tile_list_snooker_visit_board_kernel(
                 raw.rearrange("p j (m t) -> p m j t", t=PACK),
             )
 
-        def load_wg(wg, slots, name, tag=None):
-            tile = held([P, slots.stop - slots.start, S], F32, name, tag)
-            rows = wg.rearrange("(q t) s -> q t s", t=PACK)
-            for quad in range(4):
-                nc.sync.dma_start(tile[32 * quad : 32 * quad + 32], rows[:, slots, :])
+        def load_wg(wg, name):
+            tile = held([P, S], F32, name)
+            nc.sync.dma_start(tile[:], wg)
             return tile
+
+        def turn_wg(natural):
+            turned = bank()
+            for c in range(4):
+                nc.tensor.transpose(turned[:, P * c : P * (c + 1)], natural[:, P * c : P * (c + 1)], identity[:])
+            return turned
+
+        def deal_wg(turned, rows, t):
+            spread = ring([P, 4, P], F32, "spread", 2)
+            picked = turned[:].rearrange("p (c q t) -> p t c q", c=4, t=PACK)[:, t]
+            nc.scalar.copy(spread[:].rearrange("p c (r q) -> p c r q", r=4), picked.unsqueeze(2).to_broadcast([P, 4, 4, 32]))
+            back = bank()
+            for c in range(4):
+                nc.tensor.transpose(back[:, P * c : P * (c + 1)], spread[:, c, :], identity[:])
+            nc.scalar.copy(rows[:, t, :], back[:])
 
         page_rows = page0.rearrange("(a p t) c -> a t p c", a=2, t=PACK)
         pages = {}
@@ -106,60 +120,82 @@ def tile_list_snooker_visit_board_kernel(
         def scatter(u, offsets, h, wg_row):
             nc.vector.tensor_tensor(pages[u][:].indirect(offsets[:]), h[:], wg_row, ALU.mult)
 
-        t2_plane = zeroed_plane(nc.vector, TC, "t2_plane")
-        w2_plane_raw = zeroed_plane(nc.vector, KP, "w2_plane_raw")
+        t2_plane = zeroed_plane(nc.gpsimd, TC, "t2_plane")
+        w2_plane_raw = zeroed_plane(nc.gpsimd, KP, "w2_plane_raw")
+        identity = held([P, P], F32, "identity")
+        make_identity(nc, identity[:])
         tab_plane = zeroed_plane(nc.gpsimd, T, "tab_plane")
         w3_plane = zeroed_plane(nc.gpsimd, 2 * KP, "w3_plane")
 
         list2 = load_list(offs2, "list2")
+        w2_raw = [load_words(w2_words[0, :, 0:KP, :], "w2_raw0")]
+        wg2_natural = load_wg(wg2, "wg2_natural")
         t2_words = load_words(tab2_words[0], "t2_words")
         for quad in range(4):
             nc.sync.dma_start(
                 t2_plane[32 * quad : 32 * quad + 4, :].bitcast(I32),
                 tab2_scales[0, 4 * quad : 4 * quad + 4, :].bitcast(I32),
             )
-        w2_raw = [load_words(w2_words[0, :, 0:KP, :], "w2_raw0")]
         for quad in range(4):
             nc.sync.dma_start(
                 w2_plane_raw[32 * quad : 32 * quad + 8, :].bitcast(I32),
                 w2_scales[0, 4 * quad : 4 * quad + 4, :].rearrange("r (b c) -> b r c", b=2).bitcast(I32),
             )
-        list4 = load_list(offs4, "list4")
-        wg2_first = load_wg(wg2, slice(0, 1), "wg2_first")
         load_page(0)
+        list4 = load_list(offs4, "list4")
         w2_raw.append(load_words(w2_words[0, :, KP : 2 * KP, :], "w2_raw1"))
-        wg2_rest = load_wg(wg2, slice(1, 4), "wg2_rest", "wg2_then_shot")
+        wg2_rows = held([P, PACK, S], F32, "wg2_rows", "wg2_then_shot")
+        wg2_turned = turn_wg(wg2_natural)
+        deal_wg(wg2_turned, wg2_rows, 0)
 
-        v2_words = gather(t2_words[:].bitcast(U32), list2, U32, "v2_words")
-        v2_plane = gather(t2_plane[:], list2, U8, "v2_plane")
+        def deal_columns(dealt, natural):
+            nc.vector.tensor_copy(dealt[:].rearrange("p (t m) -> p m t", t=PACK), natural[:].rearrange("p (m t) -> p m t", t=PACK))
+
+        w2_dealt = [held([P, KP], I32, "w2_dealt%d" % b) for b in range(2)]
         w2_plane = held([P, KP], U8, "w2_plane")
-        nc.vector.tensor_copy(w2_plane[:].rearrange("p (t m) -> p m t", t=PACK), w2_plane_raw[:].rearrange("p (m t) -> p m t", t=PACK))
+        deal_columns(w2_dealt[0], w2_raw[0])
+        deal_columns(w2_plane, w2_plane_raw)
+        v2_words = held([P, S], U32, "v2_words")
+        v2_plane = held([P, S], U8, "v2_plane")
+        halves = [slice(0, S // 2), slice(S // 2, S)]
+        for part in halves:
+            entries = list2[:, part.start // 16 : part.stop // 16]
+            nc.vector.tensor_copy(v2_words[:, part], t2_words[:].bitcast(U32).indirect(entries))
+            nc.vector.tensor_copy(v2_plane[:, part], t2_plane[:].indirect(entries))
 
-        def cue_features(b):
-            dealt = held([P, KP], I32, "w2_dealt%d" % b)
-            nc.vector.tensor_copy(dealt[:].rearrange("p (t m) -> p m t", t=PACK), w2_raw[b][:].rearrange("p (m t) -> p m t", t=PACK))
-            tiles = []
-            for t in range(PACK):
-                cols = slice(P * t, P * (t + 1))
+        def cue_features(u, parts):
+            b, t = divmod(u, PACK)
+            cols = slice(P * t, P * (t + 1))
+            h = ring([P, S], F32, "h", 6)
+            for part in parts:
                 acc = bank()
                 nc.tensor.matmul_mx(
-                    out=acc[:], lhsT=dealt[:, cols].bitcast(FP8X4), lhsT_scale=w2_plane[4 * b :, cols],
-                    rhs=v2_words[:].bitcast(FP8X4), rhs_scale=v2_plane[:], start=True, stop=True,
+                    out=acc[:, part], lhsT=w2_dealt[b][:, cols].bitcast(FP8X4), lhsT_scale=w2_plane[4 * b :, cols],
+                    rhs=v2_words[:, part].bitcast(FP8X4), rhs_scale=v2_plane[:, part], start=True, stop=True,
                 )
-                h = ring([P, S], F32, "h", 6)
-                nc.scalar.activation(h[:], acc[:], ACT.Silu)
-                tiles.append(h)
-            return tiles
+                nc.scalar.activation(h[:, part], acc[:, part], ACT.Silu)
+            return h
 
         def wg2_row(t):
-            return wg2_first[:, 0, :] if t == 0 else wg2_rest[:, t - 1, :]
+            return wg2_rows[:, t, :]
 
-        h2 = cue_features(0)
-        scatter(0, list4, h2[0], wg2_row(0))
-        h2 = h2 + cue_features(1)
+        whole = [slice(0, S)]
+        h2 = [cue_features(0, halves)]
+        for part in halves:
+            entries = list4[:, part.start // 16 : part.stop // 16]
+            nc.vector.tensor_tensor(pages[0][:].indirect(entries), h2[0][:, part], wg2_rows[:, 0, part], ALU.mult)
         for u in range(1, 4):
+            deal_wg(wg2_turned, wg2_rows, u)
+            h2.append(cue_features(u, whole))
             load_page(u)
             scatter(u, list4, h2[u], wg2_row(u))
+        deal_columns(w2_dealt[1], w2_raw[1])
+        h2 = h2 + [cue_features(u, whole) for u in range(4, 8)]
+
+        wg1_rows = held([P, PACK, S], F32, "wg1_rows")
+        wg1_turned = turn_wg(load_wg(wg1, "wg1_natural"))
+        for t in range(4):
+            deal_wg(wg1_turned, wg1_rows, t)
 
         list1 = load_list(offs, "list1")
         for quad in range(4):
@@ -206,7 +242,6 @@ def tile_list_snooker_visit_board_kernel(
             load_page(u)
             scatter(u, list4, h2[u], wg2_row(u - 4))
         list3 = load_list(offs3, "list3")
-        wg1_rows = load_wg(wg1, slice(0, 4), "wg1_rows")
         for u in range(4):
             scatter(u, list3, h1[u], wg1_rows[:, u, :])
 
@@ -267,22 +302,29 @@ def tile_list_snooker_visit_board_kernel(
         grouped_a = held([P, PACK * KP], BF16, "grouped_a", "a_then_picks")
         interleave(nc.scalar.copy, grouped_a[:], scaled_a[:])
 
-        def scores(x0, x0_col, x1, j0, width, n_cols):
+        def score_passes(acc, c, a, xq, base, width, n_cols):
+            for n0 in range(0, width, n_cols):
+                cols = slice(base + n0, base + n0 + n_cols)
+                nc.tensor.matmul_mx(
+                    out=acc[:, n0 : n0 + n_cols],
+                    lhsT=w3_codes[:, a, 2 * P * c : 2 * P * (c + 1)].bitcast(FP4X4),
+                    lhsT_scale=w3_view[:, a, P * c : P * (c + 1)],
+                    rhs=xq[0][:, cols].bitcast(FP8X4), rhs_scale=xq[1][:, cols],
+                    start=(a == 0 and n0 == 0), stop=(a == 1 and n0 + n_cols == width),
+                )
+
+        def open_scores(xq, base, width, n_cols):
+            banks = [bank() for c in range(4)]
+            for c in range(4):
+                score_passes(banks[c], c, 0, xq, base, width, n_cols)
+            return banks
+
+        def close_scores(banks, xq, j0, width, n_cols):
             half, col = divmod(j0, KP)
             for c in range(4):
-                acc = bank()
-                for n0 in range(0, width, n_cols):
-                    for a, (xq, base) in enumerate(((x0, x0_col), (x1, 0))):
-                        cols = slice(base + n0, base + n0 + n_cols)
-                        nc.tensor.matmul_mx(
-                            out=acc[:, n0 : n0 + n_cols],
-                            lhsT=w3_codes[:, a, 2 * P * c : 2 * P * (c + 1)].bitcast(FP4X4),
-                            lhsT_scale=w3_view[:, a, P * c : P * (c + 1)],
-                            rhs=xq[0][:, cols].bitcast(FP8X4), rhs_scale=xq[1][:, cols],
-                            start=(a == 0), stop=(a == 1),
-                        )
+                score_passes(banks[c], c, 1, xq, 0, width, n_cols)
                 shot = shots[half][:, c, col : col + width]
-                nc.vector.tensor_tensor(shot, acc[:, 0:width], shot, ALU.min)
+                nc.vector.tensor_tensor(shot, banks[c][:, 0:width], shot, ALU.min)
                 nc.sync.dma_start(out[P * c : P * (c + 1), j0 : j0 + width], shot)
 
         Q = KP // 2
@@ -294,6 +336,8 @@ def tile_list_snooker_visit_board_kernel(
         interleave(nc.scalar.copy, grouped_b[:], scaled_b[:])
 
         x0 = [quantize(grouped0[:, half, :], KP) for half in range(2)]
+        banks_a = open_scores(x0[0], 0, KP, KP)
+        banks_b = open_scores(x0[1], 0, Q, P)
         xa = quantize(grouped_a[:], KP)
 
         picks_c = held([P, PACK, Q], F32, "picks_c", "a_then_picks")
@@ -301,10 +345,11 @@ def tile_list_snooker_visit_board_kernel(
         for u in range(4, 8):
             pick(u, picks_c, scaled_c, KP + Q, Q)
 
-        scores(x0[0], 0, xa, 0, KP, KP)
+        close_scores(banks_a, xa, 0, KP, KP)
+        banks_c = open_scores(x0[1], Q, Q, P)
         xb = quantize(grouped_b[:], Q)
         grouped_c = grouped_tile([P, PACK * Q])
         interleave(nc.vector.tensor_copy, grouped_c[:], scaled_c[:])
         xc = quantize(grouped_c[:], Q)
-        scores(x0[1], 0, xb, KP, Q, P)
-        scores(x0[1], Q, xc, KP + Q, Q, P)
+        close_scores(banks_b, xb, KP, Q, P)
+        close_scores(banks_c, xc, KP + Q, Q, P)

@@ -120,28 +120,31 @@ def tile_list_snooker_visit_board_kernel(
         def scatter(u, offsets, h, wg_row):
             nc.vector.tensor_tensor(pages[u][:].indirect(offsets[:]), h[:], wg_row, ALU.mult)
 
+        warm = held([P, 2], F32, "warm")
+        nc.vector.memset(warm[:, 0:1], 0.0)
+        nc.scalar.activation(warm[:, 1:2], warm[:, 0:1], ACT.Silu)
         t2_plane = zeroed_plane(nc.gpsimd, TC, "t2_plane")
-        w2_plane_raw = zeroed_plane(nc.gpsimd, KP, "w2_plane_raw")
         identity = held([P, P], F32, "identity")
         make_identity(nc, identity[:])
+        w2_plane_raw = zeroed_plane(nc.gpsimd, KP, "w2_plane_raw")
         tab_plane = zeroed_plane(nc.gpsimd, T, "tab_plane")
         w3_plane = zeroed_plane(nc.gpsimd, 2 * KP, "w3_plane")
 
         list2 = load_list(offs2, "list2")
-        w2_raw = [load_words(w2_words[0, :, 0:KP, :], "w2_raw0")]
-        wg2_natural = load_wg(wg2, "wg2_natural")
         t2_words = load_words(tab2_words[0], "t2_words")
+        wg2_natural = load_wg(wg2, "wg2_natural")
+        w2_raw = [load_words(w2_words[0, :, 0:KP, :], "w2_raw0")]
         for quad in range(4):
             nc.sync.dma_start(
                 t2_plane[32 * quad : 32 * quad + 4, :].bitcast(I32),
                 tab2_scales[0, 4 * quad : 4 * quad + 4, :].bitcast(I32),
             )
+        load_page(0)
         for quad in range(4):
-            nc.sync.dma_start(
+            nc.scalar.dma_start(
                 w2_plane_raw[32 * quad : 32 * quad + 8, :].bitcast(I32),
                 w2_scales[0, 4 * quad : 4 * quad + 4, :].rearrange("r (b c) -> b r c", b=2).bitcast(I32),
             )
-        load_page(0)
         list4 = load_list(offs4, "list4")
         w2_raw.append(load_words(w2_words[0, :, KP : 2 * KP, :], "w2_raw1"))
         wg2_rows = held([P, PACK, S], F32, "wg2_rows", "wg2_then_shot")
@@ -153,15 +156,19 @@ def tile_list_snooker_visit_board_kernel(
 
         w2_dealt = [held([P, KP], I32, "w2_dealt%d" % b) for b in range(2)]
         w2_plane = held([P, KP], U8, "w2_plane")
-        deal_columns(w2_dealt[0], w2_raw[0])
-        deal_columns(w2_plane, w2_plane_raw)
         v2_words = held([P, S], U32, "v2_words")
         v2_plane = held([P, S], U8, "v2_plane")
         halves = [slice(0, S // 2), slice(S // 2, S)]
-        for part in halves:
+
+        def gather_cue(part):
             entries = list2[:, part.start // 16 : part.stop // 16]
             nc.vector.tensor_copy(v2_words[:, part], t2_words[:].bitcast(U32).indirect(entries))
             nc.vector.tensor_copy(v2_plane[:, part], t2_plane[:].indirect(entries))
+
+        gather_cue(halves[0])
+        deal_columns(w2_dealt[0], w2_raw[0])
+        nc.vector.tensor_copy(w2_plane[:].rearrange("p (t m) -> p t m", t=PACK), w2_plane_raw[:].rearrange("p (m t) -> p t m", t=PACK))
+        gather_cue(halves[1])
 
         def cue_features(u, parts):
             b, t = divmod(u, PACK)
@@ -298,7 +305,9 @@ def tile_list_snooker_visit_board_kernel(
         scaled_a = grouped_tile([P, PACK, KP])
         for u in range(4, 8):
             scatter(u, list3, h1[u], wg1_rows[:, u - 4, :])
-            pick(u, picks_a, scaled_a, 0, KP)
+            if u > 4:
+                pick(u - 1, picks_a, scaled_a, 0, KP)
+        pick(7, picks_a, scaled_a, 0, KP)
         grouped_a = held([P, PACK * KP], BF16, "grouped_a", "a_then_picks")
         interleave(nc.scalar.copy, grouped_a[:], scaled_a[:])
 
@@ -319,20 +328,19 @@ def tile_list_snooker_visit_board_kernel(
                 score_passes(banks[c], c, 0, xq, base, width, n_cols)
             return banks
 
-        def close_scores(banks, xq, j0, width, n_cols):
+        def close_scores(banks, xq, j0, width, n_cols, result):
             half, col = divmod(j0, KP)
             for c in range(4):
                 score_passes(banks[c], c, 1, xq, 0, width, n_cols)
-                shot = shots[half][:, c, col : col + width]
-                nc.vector.tensor_tensor(shot, banks[c][:, 0:width], shot, ALU.min)
-                nc.sync.dma_start(out[P * c : P * (c + 1), j0 : j0 + width], shot)
+                nc.vector.tensor_tensor(result[:, c, :], banks[c][:, 0:width], shots[half][:, c, col : col + width], ALU.min)
+                nc.sync.dma_start(out[P * c : P * (c + 1), j0 : j0 + width], result[:, c, :])
 
         Q = KP // 2
         picks_b = raw_tile([P, PACK, Q], F32)
         scaled_b = grouped_tile([P, PACK, Q])
         for u in range(4, 8):
             pick(u, picks_b, scaled_b, KP, Q)
-        grouped_b = grouped_tile([P, PACK * Q])
+        grouped_b = held([P, PACK * Q], BF16, "grouped_b", "w1_then_picks")
         interleave(nc.scalar.copy, grouped_b[:], scaled_b[:])
 
         x0 = [quantize(grouped0[:, half, :], KP) for half in range(2)]
@@ -345,11 +353,12 @@ def tile_list_snooker_visit_board_kernel(
         for u in range(4, 8):
             pick(u, picks_c, scaled_c, KP + Q, Q)
 
-        close_scores(banks_a, xa, 0, KP, KP)
-        banks_c = open_scores(x0[1], Q, Q, P)
+        grouped_c = held([P, PACK * Q], BF16, "grouped_c", "a_then_picks")
+        interleave(nc.scalar.copy, grouped_c[:], scaled_c[:])
+
         xb = quantize(grouped_b[:], Q)
-        grouped_c = grouped_tile([P, PACK * Q])
-        interleave(nc.vector.tensor_copy, grouped_c[:], scaled_c[:])
+        close_scores(banks_a, xa, 0, KP, KP, held([P, 4, KP], F32, "result_a", "w1_then_picks"))
+        banks_c = open_scores(x0[1], Q, Q, P)
         xc = quantize(grouped_c[:], Q)
-        close_scores(banks_b, xb, KP, Q, P)
-        close_scores(banks_c, xc, KP + Q, Q, P)
+        close_scores(banks_b, xb, KP, Q, P, held([P, 4, Q], F32, "result_b", "a_then_picks"))
+        close_scores(banks_c, xc, KP + Q, Q, P, raw_tile([P, 4, Q], F32))

from contextlib import ExitStack

import concourse.mybir as mybir
from concourse.masks import make_identity

F32 = mybir.dt.float32
BF16 = mybir.dt.bfloat16
I32 = mybir.dt.int32
U32 = mybir.dt.uint32
U16 = mybir.dt.uint16
U8 = mybir.dt.uint8
FP8X4 = mybir.dt.float8_e4m3fn_x4
FP4X4 = mybir.dt.float4_e2m1fn_x4
ACT = mybir.ActivationFunctionType
ALU = mybir.AluOpType

FLOPS = 3221225472

P = 128
PACK = 4
KP = 512
T, TC, S, T2, PJ = 2048, 1024, 512, 2048, 1024


def tile_list_snooker_visit_board_kernel(
    tc, tab_words, tab_scales, tab2_words, tab2_scales, offs, offs2, offs3, offs4, offs5,
    w1, b1, w2_words, w2_scales, wg1, wg2, page0, gain, w3_words, w3_scales, safe, w4, out,
):
    nc = tc.nc
    with ExitStack() as ctx:
        lists = ctx.enter_context(tc.tile_pool(name="lists", bufs=1))
        keep = ctx.enter_context(tc.tile_pool(name="keep", bufs=1))
        psum = ctx.enter_context(tc.psum_pool(name="psum", bufs=8))

        def load_list(src, name):
            tile = lists.tile([P, src.shape[1]], U16, name=name)
            nc.sync.dma_start(tile[:], src)
            return tile

        def held(shape, dtype, name, tag=None):
            return keep.tile(shape, dtype, name=name, tag=tag or name, bufs=1, align_bytes=64)

        def ring(shape, dtype, tag, bufs):
            return keep.tile(shape, dtype, name=tag, tag=tag, bufs=bufs, align_bytes=64)

        def raw_tile(shape, dtype):
            return ring(shape, dtype, "raw", 4)

        def grouped_tile(shape):
            return ring(shape, BF16, "grouped", 4)

        def bank():
            return psum.tile([P, KP], F32, name="bank", tag="bank")

        def zeroed_plane(engine, width, name):
            tile = held([P, width], U8, name)
            engine.memset(tile[:].bitcast(I32), 0)
            return tile

        def load_words(src, name):
            tile = held([P, src.shape[1]], I32, name)
            nc.sync.dma_start(tile[:], src.rearrange("p t i -> p (t i)").bitcast(I32))
            return tile

        def gather(window, offsets, dtype, name):
            tile = held([P, S], dtype, name)
            nc.vector.tensor_copy(tile[:], window.indirect(offsets[:]))
            return tile

        def quantize(grouped, width):
            codes = ring([P, width], U32, "codes", 5)
            scales = ring([P, width], U8, "scales", 5)
            nc.vector.quantize_mx(out=codes[:].bitcast(FP8X4), scales=scales[:], in_=grouped)
            return codes, scales

        def load_raw(src):
            raw = raw_tile([P, PACK, KP], F32)
            nc.sync.dma_start(raw[:], src.rearrange("(p j) c -> p j c", j=PACK))
            return raw

        def interleave(copy, grouped, planes):
            copy(
                grouped.rearrange("p (c i t) -> p c t i", i=4, t=PACK),
                planes.rearrange("p t (c i) -> p c t i", i=4),
            )

        def interleave_dealt(grouped, raw):
            nc.scalar.copy(
                grouped.rearrange("p (t m j) -> p m j t", t=PACK, j=PACK),
                raw.rearrange("p j (m t) -> p m j t", t=PACK),
            )

        def load_wg(wg, name):
            tile = held([P, S], F32, name)
            nc.sync.dma_start(tile[:], wg)
            return tile

        def turn_wg(natural):
            turned = bank()
            for c in range(4):
                nc.tensor.transpose(turned[:, P * c : P * (c + 1)], natural[:, P * c : P * (c + 1)], identity[:])
            return turned

        def deal_wg(turned, rows, t):
            spread = ring([P, 4, P], F32, "spread", 2)
            picked = turned[:].rearrange("p (c q t) -> p t c q", c=4, t=PACK)[:, t]
            nc.scalar.copy(spread[:].rearrange("p c (r q) -> p c r q", r=4), picked.unsqueeze(2).to_broadcast([P, 4, 4, 32]))
            back = bank()
            for c in range(4):
                nc.tensor.transpose(back[:, P * c : P * (c + 1)], spread[:, c, :], identity[:])
            nc.scalar.copy(rows[:, t, :], back[:])

        page_rows = page0.rearrange("(a p t) c -> a t p c", a=2, t=PACK)
        pages = {}

        def load_page(u):
            pages[u] = held([P, T2], F32, "page%d" % u)
            nc.sync.dma_start(pages[u][:], page_rows[u // PACK, u % PACK])

        def scatter(u, offsets, h, wg_row):
            nc.vector.tensor_tensor(pages[u][:].indirect(offsets[:]), h[:], wg_row, ALU.mult)

        warm = held([P, 2], F32, "warm")
        nc.vector.memset(warm[:, 0:1], 0.0)
        nc.scalar.activation(warm[:, 1:2], warm[:, 0:1], ACT.Silu)
        t2_plane = zeroed_plane(nc.gpsimd, TC, "t2_plane")
        identity = held([P, P], F32, "identity")
        make_identity(nc, identity[:])
        w2_plane_raw = zeroed_plane(nc.gpsimd, KP, "w2_plane_raw")
        tab_plane = zeroed_plane(nc.gpsimd, T, "tab_plane")
        w3_plane = zeroed_plane(nc.gpsimd, 2 * KP, "w3_plane")

        list2 = load_list(offs2, "list2")
        t2_words = load_words(tab2_words[0], "t2_words")
        wg2_natural = load_wg(wg2, "wg2_natural")
        w2_raw = [load_words(w2_words[0, :, 0:KP, :], "w2_raw0")]
        for quad in range(4):
            nc.sync.dma_start(
                t2_plane[32 * quad : 32 * quad + 4, :].bitcast(I32),
                tab2_scales[0, 4 * quad : 4 * quad + 4, :].bitcast(I32),
            )
        load_page(0)
        for quad in range(4):
            nc.scalar.dma_start(
                w2_plane_raw[32 * quad : 32 * quad + 8, :].bitcast(I32),
                w2_scales[0, 4 * quad : 4 * quad + 4, :].rearrange("r (b c) -> b r c", b=2).bitcast(I32),
            )
        list4 = load_list(offs4, "list4")
        w2_raw.append(load_words(w2_words[0, :, KP : 2 * KP, :], "w2_raw1"))
        wg2_rows = held([P, PACK, S], F32, "wg2_rows", "wg2_then_shot")
        wg2_turned = turn_wg(wg2_natural)
        deal_wg(wg2_turned, wg2_rows, 0)

        def deal_columns(dealt, natural):
            nc.vector.tensor_copy(dealt[:].rearrange("p (t m) -> p m t", t=PACK), natural[:].rearrange("p (m t) -> p m t", t=PACK))

        w2_dealt = [held([P, KP], I32, "w2_dealt%d" % b) for b in range(2)]
        w2_plane = held([P, KP], U8, "w2_plane")
        v2_words = held([P, S], U32, "v2_words")
        v2_plane = held([P, S], U8, "v2_plane")
        halves = [slice(0, S // 2), slice(S // 2, S)]

        def gather_cue(part):
            entries = list2[:, part.start // 16 : part.stop // 16]
            nc.vector.tensor_copy(v2_words[:, part], t2_words[:].bitcast(U32).indirect(entries))
            nc.vector.tensor_copy(v2_plane[:, part], t2_plane[:].indirect(entries))

        gather_cue(halves[0])
        deal_columns(w2_dealt[0], w2_raw[0])
        nc.vector.tensor_copy(w2_plane[:].rearrange("p (t m) -> p t m", t=PACK), w2_plane_raw[:].rearrange("p (m t) -> p t m", t=PACK))
        gather_cue(halves[1])

        def cue_features(u, parts):
            b, t = divmod(u, PACK)
            cols = slice(P * t, P * (t + 1))
            h = ring([P, S], F32, "h", 6)
            for part in parts:
                acc = bank()
                nc.tensor.matmul_mx(
                    out=acc[:, part], lhsT=w2_dealt[b][:, cols].bitcast(FP8X4), lhsT_scale=w2_plane[4 * b :, cols],
                    rhs=v2_words[:, part].bitcast(FP8X4), rhs_scale=v2_plane[:, part], start=True, stop=True,
                )
                nc.scalar.activation(h[:, part], acc[:, part], ACT.Silu)
            return h

        def wg2_row(t):
            return wg2_rows[:, t, :]

        whole = [slice(0, S)]
        h2 = [cue_features(0, halves)]
        for part in halves:
            entries = list4[:, part.start // 16 : part.stop // 16]
            nc.vector.tensor_tensor(pages[0][:].indirect(entries), h2[0][:, part], wg2_rows[:, 0, part], ALU.mult)
        for u in range(1, 4):
            deal_wg(wg2_turned, wg2_rows, u)
            h2.append(cue_features(u, whole))
            load_page(u)
            scatter(u, list4, h2[u], wg2_row(u))
        deal_columns(w2_dealt[1], w2_raw[1])
        h2 = h2 + [cue_features(u, whole) for u in range(4, 8)]

        wg1_rows = held([P, PACK, S], F32, "wg1_rows")
        wg1_turned = turn_wg(load_wg(wg1, "wg1_natural"))
        for t in range(4):
            deal_wg(wg1_turned, wg1_rows, t)

        list1 = load_list(offs, "list1")
        for quad in range(4):
            nc.sync.dma_start(
                tab_plane[32 * quad : 32 * quad + 8, :].bitcast(I32),
                tab_scales[:, 4 * quad : 4 * quad + 4, :].bitcast(I32),
            )
        v_plane = gather(tab_plane[:], list1, U8, "v_plane")
        v_words = []
        for a in range(2):
            words = load_words(tab_words[a], "tab_words%d" % a)
            v_words.append(gather(words[:].bitcast(U32), list1, U32, "v_words%d" % a))
            load_page(4 + a)
            scatter(4 + a, list4, h2[4 + a], wg2_row(a))

        bias = held([P, 2, PACK], F32, "bias")
        nc.sync.dma_start(bias[:], b1.rearrange("(a p t) -> p a t", a=2, t=PACK))

        def w1_piece(a, b, grouped):
            raw = load_raw(w1[KP * a : KP * (a + 1), KP * b : KP * (b + 1)])
            interleave_dealt(grouped, raw[:])
            return quantize(grouped, KP)

        def layout_features(b, w1q):
            tiles = []
            for t in range(PACK):
                cols = slice(P * t, P * (t + 1))
                acc = bank()
                for a in range(2):
                    codes, scales = w1q[a]
                    nc.tensor.matmul_mx(
                        out=acc[:], lhsT=codes[:, cols].bitcast(FP8X4), lhsT_scale=scales[:, cols],
                        rhs=v_words[a][:].bitcast(FP8X4), rhs_scale=v_plane[4 * a :, :],
                        start=(a == 0), stop=(a == 1),
                    )
                h = ring([P, S], F32, "h", 6)
                nc.scalar.activation(h[:], acc[:], ACT.Tanh, bias=bias[:, b, t : t + 1])
                tiles.append(h)
            return tiles

        w1q = [w1_piece(a, 0, grouped_tile([P, PACK * KP])[:]) for a in range(2)]
        h1 = layout_features(0, w1q)
        for u in range(6, 8):
            load_page(u)
            scatter(u, list4, h2[u], wg2_row(u - 4))
        list3 = load_list(offs3, "list3")
        for u in range(4):
            scatter(u, list3, h1[u], wg1_rows[:, u, :])

        def plain_piece(src):
            raw = load_raw(src)
            grouped = grouped_tile([P, PACK * KP])
            interleave(nc.scalar.copy, grouped[:], raw[:])
            return quantize(grouped[:], KP)

        w4q = plain_piece(w4)
        safeq = [plain_piece(safe[:, KP * half : KP * (half + 1)]) for half in range(2)]
        last_grouped = held([P, PACK * KP], BF16, "last_grouped", "w1_then_picks")
        w1q = [w1_piece(0, 1, grouped_tile([P, PACK * KP])[:]), w1_piece(1, 1, last_grouped[:])]

        w3_codes = held([P, 2, 2 * KP], U8, "w3_codes")
        nc.sync.dma_start(w3_codes[:].bitcast(I32), w3_words.rearrange("a p c -> p a c").bitcast(I32))
        w3_view = w3_plane[:].rearrange("p (a c) -> p a c", a=2)
        for quad in range(4):
            nc.sync.dma_start(
                w3_view[32 * quad : 32 * quad + 4].bitcast(I32),
                w3_scales[:, 4 * quad : 4 * quad + 4, :].rearrange("a r c -> r a c").bitcast(I32),
            )
        gains = held([P, 2, PACK], F32, "gains")
        nc.sync.dma_start(gains[:], gain.rearrange("(a p t) -> p a t", a=2, t=PACK))
        list5 = load_list(offs5, "list5")

        h1 = h1 + layout_features(1, w1q)

        shots = [held([P, 4, KP], F32, "shot0"), held([P, 4, KP], F32, "shot1", "wg2_then_shot")]
        for half in range(2):
            for c in range(4):
                cols = slice(P * c, P * (c + 1))
                acc = bank()
                nc.tensor.matmul_mx(
                    out=acc[:], lhsT=w4q[0][:, cols].bitcast(FP8X4), lhsT_scale=w4q[1][:, cols],
                    rhs=safeq[half][0][:].bitcast(FP8X4), rhs_scale=safeq[half][1][:], start=True, stop=True,
                )
                nc.scalar.copy(shots[half][:, c, :], acc[:])

        def pick(u, picks, scaled, j0, width):
            a, t = divmod(u, PACK)
            nc.vector.tensor_copy(picks[:, t, :], pages[u][:].indirect(list5[:, j0 // 16 : (j0 + width) // 16]))
            nc.scalar.activation(scaled[:, t, :], picks[:, t, :], ACT.Copy, scale=gains[:, a, t : t + 1])

        picks0 = held([P, PACK, PJ], F32, "picks0", "w1_then_picks")
        scaled0 = raw_tile([P, PACK, PJ], BF16)
        for u in range(4):
            pick(u, picks0, scaled0, 0, PJ)
        grouped0 = raw_tile([P, 2, PACK * KP], BF16)
        for half in range(2):
            interleave(nc.scalar.copy, grouped0[:, half, :], scaled0[:, :, KP * half : KP * (half + 1)])

        picks_a = raw_tile([P, PACK, KP], F32)
        scaled_a = grouped_tile([P, PACK, KP])
        for u in range(4, 8):
            scatter(u, list3, h1[u], wg1_rows[:, u - 4, :])
            if u > 4:
                pick(u - 1, picks_a, scaled_a, 0, KP)
        pick(7, picks_a, scaled_a, 0, KP)
        grouped_a = held([P, PACK * KP], BF16, "grouped_a", "a_then_picks")
        interleave(nc.scalar.copy, grouped_a[:], scaled_a[:])

        def score_passes(acc, c, a, xq, base, width, n_cols):
            for n0 in range(0, width, n_cols):
                cols = slice(base + n0, base + n0 + n_cols)
                nc.tensor.matmul_mx(
                    out=acc[:, n0 : n0 + n_cols],
                    lhsT=w3_codes[:, a, 2 * P * c : 2 * P * (c + 1)].bitcast(FP4X4),
                    lhsT_scale=w3_view[:, a, P * c : P * (c + 1)],
                    rhs=xq[0][:, cols].bitcast(FP8X4), rhs_scale=xq[1][:, cols],
                    start=(a == 0 and n0 == 0), stop=(a == 1 and n0 + n_cols == width),
                )

        def open_scores(xq, base, width, n_cols):
            banks = [bank() for c in range(4)]
            for c in range(4):
                score_passes(banks[c], c, 0, xq, base, width, n_cols)
            return banks

        def close_scores(banks, xq, j0, width, n_cols, result):
            half, col = divmod(j0, KP)
            for c in range(4):
                score_passes(banks[c], c, 1, xq, 0, width, n_cols)
                nc.vector.tensor_tensor(result[:, c, :], banks[c][:, 0:width], shots[half][:, c, col : col + width], ALU.min)
                nc.sync.dma_start(out[P * c : P * (c + 1), j0 : j0 + width], result[:, c, :])

        Q = KP // 2
        picks_b = raw_tile([P, PACK, Q], F32)
        scaled_b = grouped_tile([P, PACK, Q])
        for u in range(4, 8):
            pick(u, picks_b, scaled_b, KP, Q)
        grouped_b = held([P, PACK * Q], BF16, "grouped_b", "w1_then_picks")
        interleave(nc.scalar.copy, grouped_b[:], scaled_b[:])

        x0 = [quantize(grouped0[:, half, :], KP) for half in range(2)]
        banks_a = open_scores(x0[0], 0, KP, KP)
        banks_b = open_scores(x0[1], 0, Q, P)
        xa = quantize(grouped_a[:], KP)

        picks_c = held([P, PACK, Q], F32, "picks_c", "a_then_picks")
        scaled_c = grouped_tile([P, PACK, Q])
        for u in range(4, 8):
            pick(u, picks_c, scaled_c, KP + Q, Q)

        grouped_c = held([P, PACK * Q], BF16, "grouped_c", "a_then_picks")
        interleave(nc.scalar.copy, grouped_c[:], scaled_c[:])

        xb = quantize(grouped_b[:], Q)
        close_scores(banks_a, xa, 0, KP, KP, held([P, 4, KP], F32, "result_a", "w1_then_picks"))
        banks_c = open_scores(x0[1], Q, Q, P)
        xc = quantize(grouped_c[:], Q)
        close_scores(banks_b, xb, KP, Q, P, held([P, 4, Q], F32, "result_b", "a_then_picks"))
        close_scores(banks_c, xc, KP + Q, Q, P, raw_tile([P, 4, Q], F32))
